import numpy as np
import ml_dtypes


def mxq(x, axis, fmt="e4m3"):
    dtype, down = {"e4m3": (ml_dtypes.float8_e4m3fn, 7), "e5m2": (ml_dtypes.float8_e5m2, 14)}[fmt]
    v = np.moveaxis(np.asarray(x, np.float32).astype(ml_dtypes.bfloat16).astype(np.float64), axis, -1)
    blocks = v.reshape(v.shape[:-1] + (-1, 32))
    amax = np.abs(blocks).max(-1, keepdims=True)
    byte = np.maximum(np.where(amax > 0, np.frexp(amax)[1] - 1 + 127, 0) - down, 1)
    scale = np.exp2(byte - 127.0)
    codes = (blocks / scale).astype(np.float32).astype(dtype).astype(np.float64)
    return np.moveaxis((codes * scale).reshape(v.shape), -1, axis)


WIDE = False


def mx_kscale(k):
    if not WIDE:
        return np.ones(k)
    levels = np.array([10, -10, 5, -5, 0])
    if k % 512:
        return np.exp2(np.random.permutation(np.resize(levels, k // 32))).repeat(32)
    a = np.empty((k // 512, 16))
    for p in range(k // 512):
        a[p, :8] = np.random.permutation(np.resize(levels, 8))
        for g in range(8):
            far = levels[np.abs(levels - a[p, g]) >= 10]
            a[p, g + 8] = far[np.random.randint(len(far))]
    return np.exp2(a.ravel()).repeat(32)


def f64(x):
    return np.asarray(x).astype(np.float64)


def striped(idx):
    return np.tile(np.asarray(idx).reshape(-1, 16).T, (8, 1)).astype(np.uint16)


def unstriped(offs):
    return offs[:16].T.reshape(-1).astype(np.int64)


E2M1 = np.array([0.0, 0.5, 1.0, 1.5, 2.0, 3.0, 4.0, 6.0, -0.0, -0.5, -1.0, -1.5, -2.0, -3.0, -4.0, -6.0])


def pack_weight(w, fmt):
    k, n = w.shape
    w = f64(np.asarray(w, np.float32).astype(ml_dtypes.bfloat16)).reshape(k // 32, 32, n)
    amax = np.abs(w).max(1)
    if fmt == "e4m3":
        byte = np.frexp(amax)[1] - 1 + 127 - 7
    else:
        mant, ex = np.frexp(amax / 6.0)
        byte = np.where(mant > 0.5, ex, ex - 1) + 127
    byte = np.clip(np.where(amax > 0, byte, 1), 1, 254)
    scaled = (w * np.exp2(127.0 - byte)[:, None, :]).reshape(k, n).astype(np.float32)
    by_word = np.ascontiguousarray(scaled.reshape(k // 512, 128, 4, n).transpose(0, 1, 3, 2))
    if fmt == "e4m3":
        words = by_word.astype(ml_dtypes.float8_e4m3fn).view(np.uint8)
    else:
        c = by_word.astype(ml_dtypes.float4_e2m1fn).view(np.uint8) & 0xF
        words = (c[..., 0::2] | (c[..., 1::2] << 4)).reshape(k // 512, 128, 2 * n)
    return np.ascontiguousarray(words), np.ascontiguousarray(byte.astype(np.uint8).reshape(k // 512, 16, n))


def unpack_weight(words, scales, fmt):
    g, _, n = scales.shape
    words = np.ascontiguousarray(words).reshape(g, 128, n, -1)
    if fmt == "e4m3":
        vals = words.view(ml_dtypes.float8_e4m3fn).astype(np.float64)
    else:
        nib = np.empty((g, 128, n, 4), np.uint8)
        nib[..., 0::2] = words & 0xF
        nib[..., 1::2] = words >> 4
        vals = E2M1[nib]
    vals = vals * np.repeat(np.exp2(scales.astype(np.float64) - 127.0), 8, axis=1)[..., None]
    return vals.transpose(0, 1, 3, 2).reshape(g * 512, n)


B, N, T, D, NQ = 1, 512, 2048, 512, 256
SEG = 16


def setup_inputs():
    n = np.random.standard_normal
    idx = np.random.permutation(T)[:B * N]
    s = mx_kscale(D)[:, None]
    mid = n((D, T))
    kp = pack_weight((mid + np.abs(n((D, T)))) / s, "e4m3")
    cp = pack_weight((mid - np.abs(n((D, T)))) / s, "e4m3")
    return {
        "qT": (n((B, D, NQ)) * s * (0.10 / np.sqrt(D))).astype(np.float32),
        "k_words": kp[0],
        "k_scales": kp[1],
        "c_words": cp[0],
        "c_scales": cp[1],
        "offs": striped(idx),
    }


def reference(qT, k_words, k_scales, c_words, c_scales, offs):
    idx = unstriped(offs)
    pick = lambda x, which: x[:, which].reshape(x.shape[0], B, -1).transpose(1, 0, 2)
    k = unpack_weight(k_words, k_scales, "e4m3")
    kg = pick(k, idx)
    c = unpack_weight(c_words, c_scales, "e4m3")
    cg = pick(c, idx)
    hiq = mxq(np.maximum(f64(qT), 0.0), 1, "e4m3")
    loq = mxq(np.minimum(f64(qT), 0.0), 1, "e4m3")
    a = (hiq.transpose(0, 2, 1) @ kg) + (loq.transpose(0, 2, 1) @ cg)
    y = np.log(np.exp(a).reshape(B, NQ, N // SEG, SEG).sum(-1))
    return y

@@ -1,0 +1,108 @@
+from contextlib import ExitStack
+
+import concourse.mybir as mybir
+
+D, T, N, NQ, SEG = 512, 2048, 512, 256, 16
+FLOPS = 2 * 2 * NQ * D * N
+
+F32 = mybir.dt.float32
+BF16 = mybir.dt.bfloat16
+I32 = mybir.dt.int32
+U32 = mybir.dt.uint32
+U16 = mybir.dt.uint16
+U8 = mybir.dt.uint8
+FP8X4 = mybir.dt.float8_e4m3fn_x4
+ALU = mybir.AluOpType
+ACT = mybir.ActivationFunctionType
+AX = mybir.AxisListType
+
+P = 128
+PACK = 4
+Q_TILES = NQ // P
+HALVES = 2
+HALF = N // HALVES
+RUNS = N // SEG
+RUNS_HALF = HALF // SEG
+C_ROW = 4
+
+
+def tile_attend_questlse_topk_kernel(tc, qT, k_words, k_scales, c_words, c_scales, offs, out):
+    nc = tc.nc
+    with ExitStack() as ctx:
+        sb = ctx.enter_context(tc.tile_pool(name="sb", bufs=1))
+        ps = ctx.enter_context(tc.psum_pool(name="ps", bufs=1))
+
+        offsets = sb.tile([P, N // 16], U16, name="offsets")
+        q_raw = sb.tile([P, PACK, NQ], F32, name="q_raw")
+        kw_all = sb.tile([P, T], I32, name="kw_all", align_bytes=64)
+        cw_all = sb.tile([P, T], I32, name="cw_all", align_bytes=64)
+        ks_all = sb.tile([P, T], U8, name="ks_all", align_bytes=64)
+        cs_all = sb.tile([P, T], U8, name="cs_all", align_bytes=64)
+
+        nc.vector.memset(cs_all[:].bitcast(I32), 0)
+        nc.vector.memset(ks_all[:].bitcast(I32), 0)
+        nc.sync.dma_start(q_raw[:], qT[0].rearrange("(p j) w -> p j w", j=PACK))
+        nc.sync.dma_start(offsets[:], offs)
+        for r in range(4):
+            nc.scalar.dma_start(ks_all[r:P:32, :].bitcast(I32), k_scales[0, r:16:4, :].bitcast(I32))
+        for r in range(4):
+            nc.gpsimd.dma_start(cs_all[C_ROW + r:P:32, :].bitcast(I32), c_scales[0, r:16:4, :].bitcast(I32))
+        nc.sync.dma_start(kw_all[:], k_words[0].rearrange("p t r -> p (t r)").bitcast(I32))
+        nc.sync.dma_start(cw_all[:], c_words[0].rearrange("p t r -> p (t r)").bitcast(I32))
+
+        hi = sb.tile([P, NQ, PACK], BF16, name="hi", align_bytes=64)
+        lo = sb.tile([P, NQ, PACK], BF16, name="lo", align_bytes=64)
+        q_read = q_raw[:].rearrange("p j (c i) -> p c j i", i=4)
+        nc.scalar.activation(hi[:].rearrange("p (c i) j -> p c j i", i=4), q_read, ACT.Relu)
+        nc.vector.tensor_scalar(lo[:].rearrange("p (c i) j -> p c j i", i=4), q_read, 0.0, None, ALU.min)
+
+        ks = sb.tile([P, N], U8, name="ks", align_bytes=64)
+        cs = sb.tile([P, N], U8, name="cs", align_bytes=64)
+        kw = sb.tile([P, N], U32, name="kw", align_bytes=64)
+        cw = sb.tile([P, N], U32, name="cw", align_bytes=64)
+        hi_w = sb.tile([P, NQ], U32, name="hi_w", align_bytes=64)
+        hi_s = sb.tile([P, NQ], U8, name="hi_s", align_bytes=64)
+        lo_w = sb.tile([P, NQ], U32, name="lo_w", align_bytes=64)
+        lo_s = sb.tile([P, NQ], U8, name="lo_s", align_bytes=64)
+
+        nc.vector.tensor_copy(ks[:], ks_all[:].indirect(offsets[:]))
+        nc.vector.quantize_mx(out=lo_w[:].bitcast(FP8X4), scales=lo_s[:], in_=lo[:].rearrange("p w j -> p (w j)"))
+        nc.vector.quantize_mx(out=hi_w[:].bitcast(FP8X4), scales=hi_s[:], in_=hi[:].rearrange("p w j -> p (w j)"))
+        nc.vector.tensor_copy(kw[:], kw_all[:].bitcast(U32).indirect(offsets[:]))
+        nc.vector.tensor_copy(cs[:], cs_all[:].indirect(offsets[:]))
+
+        blocks = [(h, t) for h in range(HALVES) for t in range(Q_TILES)]
+        acc = {b: ps.tile([P, HALF], F32, name="acc%d%d" % b) for b in blocks}
+        for h, t in blocks:
+            qs = slice(t * P, (t + 1) * P)
+            ns = slice(h * HALF, (h + 1) * HALF)
+            nc.tensor.matmul_mx(out=acc[h, t][:], lhsT=hi_w[:, qs].bitcast(FP8X4), lhsT_scale=hi_s[:, qs],
+                                rhs=kw[:, ns].bitcast(FP8X4), rhs_scale=ks[:, ns], start=True, stop=False)
+        for h in range(HALVES):
+            ns = slice(h * HALF, (h + 1) * HALF)
+            nc.vector.tensor_copy(cw[:, ns], cw_all[:].bitcast(U32).indirect(offsets[:, h * HALF // 16:(h + 1) * HALF // 16]))
+            for t in range(Q_TILES):
+                qs = slice(t * P, (t + 1) * P)
+                nc.tensor.matmul_mx(out=acc[h, t][:], lhsT=lo_w[:, qs].bitcast(FP8X4), lhsT_scale=lo_s[:, qs],
+                                    rhs=cw[:, ns].bitcast(FP8X4), rhs_scale=cs[C_ROW:, ns], start=False, stop=True)
+
+        top = sb.tile([P, Q_TILES, RUNS], F32, name="top")
+        total = sb.tile([P, Q_TILES, RUNS], F32, name="total")
+        shifted = {b: sb.tile([P, RUNS_HALF, SEG], F32, name="shifted%d%d" % b) for b in blocks}
+        weight = {b: sb.tile([P, RUNS_HALF, SEG], F32, name="weight%d%d" % b) for b in blocks}
+        for h in range(HALVES):
+            js = slice(h * RUNS_HALF, (h + 1) * RUNS_HALF)
+            for t in range(Q_TILES):
+                nc.vector.tensor_reduce(top[:, t, js], acc[h, t][:].rearrange("p (j s) -> p j s", s=SEG), AX.X, ALU.max)
+            for t in range(Q_TILES):
+                nc.vector.tensor_tensor(shifted[h, t][:], acc[h, t][:].rearrange("p (j s) -> p j s", s=SEG),
+                                        top[:, t, js].unsqueeze(2).to_broadcast([P, RUNS_HALF, SEG]), ALU.subtract)
+                nc.scalar.activation(weight[h, t][:], shifted[h, t][:], ACT.Exp)
+        for h, t in blocks:
+            js = slice(h * RUNS_HALF, (h + 1) * RUNS_HALF)
+            nc.vector.tensor_reduce(total[:, t, js], weight[h, t][:], AX.X, ALU.add)
+        logs = sb.tile([P, Q_TILES, RUNS], F32, name="logs")
+        result = sb.tile([P, Q_TILES, RUNS], F32, name="result")
+        nc.scalar.activation(logs[:], total[:], ACT.Ln)
+        nc.vector.tensor_tensor(result[:], logs[:], top[:], ALU.add)
+        nc.sync.dma_start(out[0].rearrange("(t p) j -> p t j", p=P), result[:])

@@ -39,15 +39,15 @@ def tile_attend_questlse_topk_kernel(tc, qT, k_words, k_scales, c_words, c_scale
         ks_all = sb.tile([P, T], U8, name="ks_all", align_bytes=64)
         cs_all = sb.tile([P, T], U8, name="cs_all", align_bytes=64)
 
-        nc.vector.memset(cs_all[:].bitcast(I32), 0)
         nc.vector.memset(ks_all[:].bitcast(I32), 0)
+        nc.vector.memset(cs_all[:].bitcast(I32), 0)
         nc.sync.dma_start(q_raw[:], qT[0].rearrange("(p j) w -> p j w", j=PACK))
         nc.sync.dma_start(offsets[:], offs)
         for r in range(4):
-            nc.scalar.dma_start(ks_all[r:P:32, :].bitcast(I32), k_scales[0, r:16:4, :].bitcast(I32))
-        for r in range(4):
-            nc.gpsimd.dma_start(cs_all[C_ROW + r:P:32, :].bitcast(I32), c_scales[0, r:16:4, :].bitcast(I32))
+            nc.sync.dma_start(ks_all[r:P:32, :].bitcast(I32), k_scales[0, r:16:4, :].bitcast(I32))
         nc.sync.dma_start(kw_all[:], k_words[0].rearrange("p t r -> p (t r)").bitcast(I32))
+        for r in range(4):
+            nc.sync.dma_start(cs_all[C_ROW + r:P:32, :].bitcast(I32), c_scales[0, r:16:4, :].bitcast(I32))
         nc.sync.dma_start(cw_all[:], c_words[0].rearrange("p t r -> p (t r)").bitcast(I32))
 
         hi = sb.tile([P, NQ, PACK], BF16, name="hi", align_bytes=64)
@@ -68,7 +68,9 @@ def tile_attend_questlse_topk_kernel(tc, qT, k_words, k_scales, c_words, c_scale
         nc.vector.tensor_copy(ks[:], ks_all[:].indirect(offsets[:]))
         nc.vector.quantize_mx(out=lo_w[:].bitcast(FP8X4), scales=lo_s[:], in_=lo[:].rearrange("p w j -> p (w j)"))
         nc.vector.quantize_mx(out=hi_w[:].bitcast(FP8X4), scales=hi_s[:], in_=hi[:].rearrange("p w j -> p (w j)"))
-        nc.vector.tensor_copy(kw[:], kw_all[:].bitcast(U32).indirect(offsets[:]))
+        for h in range(HALVES):
+            nc.vector.tensor_copy(kw[:, h * HALF:(h + 1) * HALF],
+                                  kw_all[:].bitcast(U32).indirect(offsets[:, h * HALF // 16:(h + 1) * HALF // 16]))
         nc.vector.tensor_copy(cs[:], cs_all[:].indirect(offsets[:]))
 
         blocks = [(h, t) for h in range(HALVES) for t in range(Q_TILES)]
@@ -88,21 +90,26 @@ def tile_attend_questlse_topk_kernel(tc, qT, k_words, k_scales, c_words, c_scale
 
         top = sb.tile([P, Q_TILES, RUNS], F32, name="top")
         total = sb.tile([P, Q_TILES, RUNS], F32, name="total")
-        shifted = {b: sb.tile([P, RUNS_HALF, SEG], F32, name="shifted%d%d" % b) for b in blocks}
+        shifted = {b: sb.tile([P, RUNS_HALF, SEG], F32, name="shifted%d%d" % b) for b in blocks[1:]}
         weight = {b: sb.tile([P, RUNS_HALF, SEG], F32, name="weight%d%d" % b) for b in blocks}
+        runs = {b: acc[b][:].rearrange("p (j s) -> p j s", s=SEG) for b in blocks}
         for h in range(HALVES):
             js = slice(h * RUNS_HALF, (h + 1) * RUNS_HALF)
             for t in range(Q_TILES):
-                nc.vector.tensor_reduce(top[:, t, js], acc[h, t][:].rearrange("p (j s) -> p j s", s=SEG), AX.X, ALU.max)
+                nc.vector.tensor_reduce(top[:, t, js], runs[h, t], AX.X, ALU.max, negate=True)
+                if (h, t) == blocks[0]:
+                    for j in range(RUNS_HALF):
+                        nc.scalar.activation(weight[h, t][:, j, :], runs[h, t][:, j, :], ACT.Exp, bias=top[:, t, j:j + 1])
             for t in range(Q_TILES):
-                nc.vector.tensor_tensor(shifted[h, t][:], acc[h, t][:].rearrange("p (j s) -> p j s", s=SEG),
-                                        top[:, t, js].unsqueeze(2).to_broadcast([P, RUNS_HALF, SEG]), ALU.subtract)
-                nc.scalar.activation(weight[h, t][:], shifted[h, t][:], ACT.Exp)
+                if (h, t) != blocks[0]:
+                    nc.vector.tensor_tensor(shifted[h, t][:], runs[h, t],
+                                            top[:, t, js].unsqueeze(2).to_broadcast([P, RUNS_HALF, SEG]), ALU.add)
+                    nc.scalar.activation(weight[h, t][:], shifted[h, t][:], ACT.Exp)
         for h, t in blocks:
             js = slice(h * RUNS_HALF, (h + 1) * RUNS_HALF)
             nc.vector.tensor_reduce(total[:, t, js], weight[h, t][:], AX.X, ALU.add)
         logs = sb.tile([P, Q_TILES, RUNS], F32, name="logs")
         result = sb.tile([P, Q_TILES, RUNS], F32, name="result")
         nc.scalar.activation(logs[:], total[:], ACT.Ln)
-        nc.vector.tensor_tensor(result[:], logs[:], top[:], ALU.add)
+        nc.vector.tensor_tensor(result[:], logs[:], top[:], ALU.subtract)
         nc.sync.dma_start(out[0].rearrange("(t p) j -> p t j", p=P), result[:])

@@ -24,6 +24,7 @@ HALF = N // HALVES
 RUNS = N // SEG
 RUNS_HALF = HALF // SEG
 C_ROW = 4
+C_FIRST = 512
 
 
 def tile_attend_questlse_topk_kernel(tc, qT, k_words, k_scales, c_words, c_scales, offs, out):
@@ -36,7 +37,7 @@ def tile_attend_questlse_topk_kernel(tc, qT, k_words, k_scales, c_words, c_scale
         q_raw = sb.tile([P, PACK, NQ], F32, name="q_raw")
         kw_all = sb.tile([P, T], I32, name="kw_all", align_bytes=64)
         cw_all = sb.tile([P, T], I32, name="cw_all", align_bytes=64)
-        ks_all = sb.tile([P, T], U8, name="ks_all", align_bytes=64)
+        ks_all = sb.tile([P, T], U8, name="ks_all", tag="shared", align_bytes=64)
         cs_all = sb.tile([P, T], U8, name="cs_all", align_bytes=64)
 
         nc.vector.memset(ks_all[:].bitcast(I32), 0)
@@ -46,9 +47,11 @@ def tile_attend_questlse_topk_kernel(tc, qT, k_words, k_scales, c_words, c_scale
         for r in range(4):
             nc.sync.dma_start(ks_all[r:P:32, :].bitcast(I32), k_scales[0, r:16:4, :].bitcast(I32))
         nc.sync.dma_start(kw_all[:], k_words[0].rearrange("p t r -> p (t r)").bitcast(I32))
+        c_src = c_words[0].rearrange("p t r -> p (t r)").bitcast(I32)
+        nc.sync.dma_start(cw_all[:, :C_FIRST], c_src[:, :C_FIRST])
         for r in range(4):
             nc.sync.dma_start(cs_all[C_ROW + r:P:32, :].bitcast(I32), c_scales[0, r:16:4, :].bitcast(I32))
-        nc.sync.dma_start(cw_all[:], c_words[0].rearrange("p t r -> p (t r)").bitcast(I32))
+        nc.sync.dma_start(cw_all[:, C_FIRST:], c_src[:, C_FIRST:])
 
         hi = sb.tile([P, NQ, PACK], BF16, name="hi", align_bytes=64)
         lo = sb.tile([P, NQ, PACK], BF16, name="lo", align_bytes=64)
@@ -60,14 +63,14 @@ def tile_attend_questlse_topk_kernel(tc, qT, k_words, k_scales, c_words, c_scale
         cs = sb.tile([P, N], U8, name="cs", align_bytes=64)
         kw = sb.tile([P, N], U32, name="kw", align_bytes=64)
         cw = sb.tile([P, N], U32, name="cw", align_bytes=64)
-        hi_w = sb.tile([P, NQ], U32, name="hi_w", align_bytes=64)
         hi_s = sb.tile([P, NQ], U8, name="hi_s", align_bytes=64)
-        lo_w = sb.tile([P, NQ], U32, name="lo_w", align_bytes=64)
         lo_s = sb.tile([P, NQ], U8, name="lo_s", align_bytes=64)
 
         nc.vector.tensor_copy(ks[:], ks_all[:].indirect(offsets[:]))
-        nc.vector.quantize_mx(out=lo_w[:].bitcast(FP8X4), scales=lo_s[:], in_=lo[:].rearrange("p w j -> p (w j)"))
-        nc.vector.quantize_mx(out=hi_w[:].bitcast(FP8X4), scales=hi_s[:], in_=hi[:].rearrange("p w j -> p (w j)"))
+        q_w = sb.tile([P, 2, NQ], U32, name="q_w", tag="shared", align_bytes=64)
+        hi_w, lo_w = q_w[:, 0, :], q_w[:, 1, :]
+        nc.vector.quantize_mx(out=lo_w.bitcast(FP8X4), scales=lo_s[:], in_=lo[:].rearrange("p w j -> p (w j)"))
+        nc.vector.quantize_mx(out=hi_w.bitcast(FP8X4), scales=hi_s[:], in_=hi[:].rearrange("p w j -> p (w j)"))
         for h in range(HALVES):
             nc.vector.tensor_copy(kw[:, h * HALF:(h + 1) * HALF],
                                   kw_all[:].bitcast(U32).indirect(offsets[:, h * HALF // 16:(h + 1) * HALF // 16]))

@@ -24,7 +24,7 @@ HALF = N // HALVES
 RUNS = N // SEG
 RUNS_HALF = HALF // SEG
 C_ROW = 4
-C_FIRST = 512
+K_FIRST = 512
 
 
 def tile_attend_questlse_topk_kernel(tc, qT, k_words, k_scales, c_words, c_scales, offs, out):
@@ -34,24 +34,34 @@ def tile_attend_questlse_topk_kernel(tc, qT, k_words, k_scales, c_words, c_scale
         ps = ctx.enter_context(tc.psum_pool(name="ps", bufs=1))
 
         offsets = sb.tile([P, N // 16], U16, name="offsets")
-        q_raw = sb.tile([P, PACK, NQ], F32, name="q_raw")
+        q_raw = sb.tile([P, PACK, NQ], F32, name="q_raw", tag="shared", align_bytes=64)
         kw_all = sb.tile([P, T], I32, name="kw_all", align_bytes=64)
         cw_all = sb.tile([P, T], I32, name="cw_all", align_bytes=64)
-        ks_all = sb.tile([P, T], U8, name="ks_all", tag="shared", align_bytes=64)
+        ks_all = sb.tile([P, T], U8, name="ks_all", align_bytes=64)
         cs_all = sb.tile([P, T], U8, name="cs_all", align_bytes=64)
 
-        nc.vector.memset(ks_all[:].bitcast(I32), 0)
+        cs_g = sb.tile([P, N], U8, name="cs_g", align_bytes=64)
+        cs = sb.tile([P, N], U8, name="cs", align_bytes=64)
+
         nc.vector.memset(cs_all[:].bitcast(I32), 0)
-        nc.sync.dma_start(q_raw[:], qT[0].rearrange("(p j) w -> p j w", j=PACK))
+        nc.vector.memset(ks_all[:].bitcast(I32), 0)
+        nc.vector.memset(cs[:].bitcast(I32), 0)
+        k_src = k_words[0].rearrange("p t r -> p (t r)").bitcast(I32)
         nc.sync.dma_start(offsets[:], offs)
+        nc.sync.dma_start(kw_all[:, :K_FIRST], k_src[:, :K_FIRST])
+        nc.sync.dma_start(cs_all[C_ROW:P:8, :].bitcast(I32), c_scales[0].bitcast(I32))
+        nc.sync.dma_start(q_raw[:], qT[0].rearrange("(p j) w -> p j w", j=PACK))
         for r in range(4):
             nc.sync.dma_start(ks_all[r:P:32, :].bitcast(I32), k_scales[0, r:16:4, :].bitcast(I32))
-        nc.sync.dma_start(kw_all[:], k_words[0].rearrange("p t r -> p (t r)").bitcast(I32))
-        c_src = c_words[0].rearrange("p t r -> p (t r)").bitcast(I32)
-        nc.sync.dma_start(cw_all[:, :C_FIRST], c_src[:, :C_FIRST])
+        nc.sync.dma_start(kw_all[:, K_FIRST:], k_src[:, K_FIRST:])
+        nc.sync.dma_start(cw_all[:], c_words[0].rearrange("p t r -> p (t r)").bitcast(I32))
+
+        nc.vector.tensor_copy(cs_g[:], cs_all[:].indirect(offsets[:]))
         for r in range(4):
-            nc.sync.dma_start(cs_all[C_ROW + r:P:32, :].bitcast(I32), c_scales[0, r:16:4, :].bitcast(I32))
-        nc.sync.dma_start(cw_all[:, C_FIRST:], c_src[:, C_FIRST:])
+            nc.sync.dma_start(cs[C_ROW + r:P:32, :].bitcast(I32), cs_g[C_ROW + 8 * r:P:32, :].bitcast(I32))
+
+        ks = sb.tile([P, N], U8, name="ks", align_bytes=64)
+        nc.vector.tensor_copy(ks[:], ks_all[:].indirect(offsets[:]))
 
         hi = sb.tile([P, NQ, PACK], BF16, name="hi", align_bytes=64)
         lo = sb.tile([P, NQ, PACK], BF16, name="lo", align_bytes=64)
@@ -59,22 +69,18 @@ def tile_attend_questlse_topk_kernel(tc, qT, k_words, k_scales, c_words, c_scale
         nc.scalar.activation(hi[:].rearrange("p (c i) j -> p c j i", i=4), q_read, ACT.Relu)
         nc.vector.tensor_scalar(lo[:].rearrange("p (c i) j -> p c j i", i=4), q_read, 0.0, None, ALU.min)
 
-        ks = sb.tile([P, N], U8, name="ks", align_bytes=64)
-        cs = sb.tile([P, N], U8, name="cs", align_bytes=64)
         kw = sb.tile([P, N], U32, name="kw", align_bytes=64)
         cw = sb.tile([P, N], U32, name="cw", align_bytes=64)
         hi_s = sb.tile([P, NQ], U8, name="hi_s", align_bytes=64)
         lo_s = sb.tile([P, NQ], U8, name="lo_s", align_bytes=64)
 
-        nc.vector.tensor_copy(ks[:], ks_all[:].indirect(offsets[:]))
-        q_w = sb.tile([P, 2, NQ], U32, name="q_w", tag="shared", align_bytes=64)
-        hi_w, lo_w = q_w[:, 0, :], q_w[:, 1, :]
-        nc.vector.quantize_mx(out=lo_w.bitcast(FP8X4), scales=lo_s[:], in_=lo[:].rearrange("p w j -> p (w j)"))
-        nc.vector.quantize_mx(out=hi_w.bitcast(FP8X4), scales=hi_s[:], in_=hi[:].rearrange("p w j -> p (w j)"))
+        hi_w = sb.tile([P, NQ], U32, name="hi_w", align_bytes=64)
+        lo_w = sb.tile([P, NQ], U32, name="lo_w", tag="shared", align_bytes=64)
+        nc.vector.quantize_mx(out=hi_w[:].bitcast(FP8X4), scales=hi_s[:], in_=hi[:].rearrange("p w j -> p (w j)"))
+        nc.vector.quantize_mx(out=lo_w[:].bitcast(FP8X4), scales=lo_s[:], in_=lo[:].rearrange("p w j -> p (w j)"))
         for h in range(HALVES):
             nc.vector.tensor_copy(kw[:, h * HALF:(h + 1) * HALF],
                                   kw_all[:].bitcast(U32).indirect(offsets[:, h * HALF // 16:(h + 1) * HALF // 16]))
-        nc.vector.tensor_copy(cs[:], cs_all[:].indirect(offsets[:]))
 
         blocks = [(h, t) for h in range(HALVES) for t in range(Q_TILES)]
         acc = {b: ps.tile([P, HALF], F32, name="acc%d%d" % b) for b in blocks}

@@ -24,6 +24,7 @@ HALF = N // HALVES
 RUNS = N // SEG
 RUNS_HALF = HALF // SEG
 C_ROW = 4
+BIAS_BLOCK = (0, 1)
 K_FIRST = 512
 
 
@@ -99,18 +100,18 @@ def tile_attend_questlse_topk_kernel(tc, qT, k_words, k_scales, c_words, c_scale
 
         top = sb.tile([P, Q_TILES, RUNS], F32, name="top")
         total = sb.tile([P, Q_TILES, RUNS], F32, name="total")
-        shifted = {b: sb.tile([P, RUNS_HALF, SEG], F32, name="shifted%d%d" % b) for b in blocks[1:]}
+        shifted = {b: sb.tile([P, RUNS_HALF, SEG], F32, name="shifted%d%d" % b) for b in blocks if b != BIAS_BLOCK}
         weight = {b: sb.tile([P, RUNS_HALF, SEG], F32, name="weight%d%d" % b) for b in blocks}
         runs = {b: acc[b][:].rearrange("p (j s) -> p j s", s=SEG) for b in blocks}
         for h in range(HALVES):
             js = slice(h * RUNS_HALF, (h + 1) * RUNS_HALF)
             for t in range(Q_TILES):
                 nc.vector.tensor_reduce(top[:, t, js], runs[h, t], AX.X, ALU.max, negate=True)
-                if (h, t) == blocks[0]:
+                if (h, t) == BIAS_BLOCK:
                     for j in range(RUNS_HALF):
                         nc.scalar.activation(weight[h, t][:, j, :], runs[h, t][:, j, :], ACT.Exp, bias=top[:, t, j:j + 1])
             for t in range(Q_TILES):
-                if (h, t) != blocks[0]:
+                if (h, t) != BIAS_BLOCK:
                     nc.vector.tensor_tensor(shifted[h, t][:], runs[h, t],
                                             top[:, t, js].unsqueeze(2).to_broadcast([P, RUNS_HALF, SEG]), ALU.add)
                     nc.scalar.activation(weight[h, t][:], shifted[h, t][:], ACT.Exp)

@@ -66,9 +66,12 @@ def tile_attend_questlse_topk_kernel(tc, qT, k_words, k_scales, c_words, c_scale
 
         hi = sb.tile([P, NQ, PACK], BF16, name="hi", align_bytes=64)
         lo = sb.tile([P, NQ, PACK], BF16, name="lo", align_bytes=64)
-        q_read = q_raw[:].rearrange("p j (c i) -> p c j i", i=4)
-        nc.scalar.activation(hi[:].rearrange("p (c i) j -> p c j i", i=4), q_read, ACT.Relu)
-        nc.vector.tensor_scalar(lo[:].rearrange("p (c i) j -> p c j i", i=4), q_read, 0.0, None, ALU.min)
+        q_read = q_raw[:].rearrange("p j (c i t) -> p t c j i", i=2, t=Q_TILES)
+        hi_write = hi[:].rearrange("p (t c i) j -> p t c j i", i=2, t=Q_TILES)
+        lo_write = lo[:].rearrange("p (t c i) j -> p t c j i", i=2, t=Q_TILES)
+        for t in range(Q_TILES):
+            nc.scalar.activation(hi_write[:, t], q_read[:, t], ACT.Relu)
+            nc.vector.tensor_scalar(lo_write[:, t], q_read[:, t], 0.0, None, ALU.min)
 
         kw = sb.tile([P, N], U32, name="kw", align_bytes=64)
         cw = sb.tile([P, N], U32, name="cw", align_bytes=64)
@@ -122,4 +125,4 @@ def tile_attend_questlse_topk_kernel(tc, qT, k_words, k_scales, c_words, c_scale
         result = sb.tile([P, Q_TILES, RUNS], F32, name="result")
         nc.scalar.activation(logs[:], total[:], ACT.Ln)
         nc.vector.tensor_tensor(result[:], logs[:], top[:], ALU.subtract)
-        nc.sync.dma_start(out[0].rearrange("(t p) j -> p t j", p=P), result[:])
+        nc.sync.dma_start(out[0].rearrange("(p t) j -> p t j", t=Q_TILES), result[:])

@@ -35,8 +35,8 @@ def tile_attend_questlse_topk_kernel(tc, qT, k_words, k_scales, c_words, c_scale
         ps = ctx.enter_context(tc.psum_pool(name="ps", bufs=1))
 
         offsets = sb.tile([P, N // 16], U16, name="offsets")
-        q_raw = sb.tile([P, PACK, NQ], F32, name="q_raw", tag="shared", align_bytes=64)
-        kw_all = sb.tile([P, T], I32, name="kw_all", align_bytes=64)
+        q_raw = sb.tile([P, PACK, NQ], F32, name="q_raw", align_bytes=64)
+        kw_all = sb.tile([P, T], I32, name="kw_all", tag="shared", align_bytes=64)
         cw_all = sb.tile([P, T], I32, name="cw_all", align_bytes=64)
         ks_all = sb.tile([P, T], U8, name="ks_all", align_bytes=64)
         cs_all = sb.tile([P, T], U8, name="cs_all", align_bytes=64)
@@ -49,9 +49,9 @@ def tile_attend_questlse_topk_kernel(tc, qT, k_words, k_scales, c_words, c_scale
         nc.vector.memset(cs[:].bitcast(I32), 0)
         k_src = k_words[0].rearrange("p t r -> p (t r)").bitcast(I32)
         nc.sync.dma_start(offsets[:], offs)
-        nc.sync.dma_start(kw_all[:, :K_FIRST], k_src[:, :K_FIRST])
-        nc.sync.dma_start(cs_all[C_ROW:P:8, :].bitcast(I32), c_scales[0].bitcast(I32))
         nc.sync.dma_start(q_raw[:], qT[0].rearrange("(p j) w -> p j w", j=PACK))
+        nc.sync.dma_start(cs_all[C_ROW:P:8, :].bitcast(I32), c_scales[0].bitcast(I32))
+        nc.sync.dma_start(kw_all[:, :K_FIRST], k_src[:, :K_FIRST])
         for r in range(4):
             nc.sync.dma_start(ks_all[r:P:32, :].bitcast(I32), k_scales[0, r:16:4, :].bitcast(I32))
         nc.sync.dma_start(kw_all[:, K_FIRST:], k_src[:, K_FIRST:])
@@ -68,10 +68,13 @@ def tile_attend_questlse_topk_kernel(tc, qT, k_words, k_scales, c_words, c_scale
         lo = sb.tile([P, NQ, PACK], BF16, name="lo", align_bytes=64)
         q_read = q_raw[:].rearrange("p j (c i t) -> p t c j i", i=2, t=Q_TILES)
         hi_write = hi[:].rearrange("p (t c i) j -> p t c j i", i=2, t=Q_TILES)
-        lo_write = lo[:].rearrange("p (t c i) j -> p t c j i", i=2, t=Q_TILES)
+        minus_lo = sb.tile([P, NQ, PACK], BF16, name="minus_lo", align_bytes=64)
+        minus_write = minus_lo[:].rearrange("p (t c i) j -> p t c j i", i=2, t=Q_TILES)
         for t in range(Q_TILES):
             nc.scalar.activation(hi_write[:, t], q_read[:, t], ACT.Relu)
-            nc.vector.tensor_scalar(lo_write[:, t], q_read[:, t], 0.0, None, ALU.min)
+        for t in range(Q_TILES):
+            nc.scalar.activation(minus_write[:, t], q_read[:, t], ACT.Relu, scale=-1.0)
+        nc.scalar.activation(lo[:], minus_lo[:], ACT.Copy, scale=-1.0)
 
         kw = sb.tile([P, N], U32, name="kw", align_bytes=64)
         cw = sb.tile([P, N], U32, name="cw", align_bytes=64)
@@ -79,12 +82,12 @@ def tile_attend_questlse_topk_kernel(tc, qT, k_words, k_scales, c_words, c_scale
         lo_s = sb.tile([P, NQ], U8, name="lo_s", align_bytes=64)
 
         hi_w = sb.tile([P, NQ], U32, name="hi_w", align_bytes=64)
-        lo_w = sb.tile([P, NQ], U32, name="lo_w", tag="shared", align_bytes=64)
         nc.vector.quantize_mx(out=hi_w[:].bitcast(FP8X4), scales=hi_s[:], in_=hi[:].rearrange("p w j -> p (w j)"))
-        nc.vector.quantize_mx(out=lo_w[:].bitcast(FP8X4), scales=lo_s[:], in_=lo[:].rearrange("p w j -> p (w j)"))
         for h in range(HALVES):
             nc.vector.tensor_copy(kw[:, h * HALF:(h + 1) * HALF],
                                   kw_all[:].bitcast(U32).indirect(offsets[:, h * HALF // 16:(h + 1) * HALF // 16]))
+        lo_w = sb.tile([P, NQ], U32, name="lo_w", tag="shared", align_bytes=64)
+        nc.vector.quantize_mx(out=lo_w[:].bitcast(FP8X4), scales=lo_s[:], in_=lo[:].rearrange("p w j -> p (w j)"))
 
         blocks = [(h, t) for h in range(HALVES) for t in range(Q_TILES)]
         acc = {b: ps.tile([P, HALF], F32, name="acc%d%d" % b) for b in blocks}

@@ -24,8 +24,11 @@ HALF = N // HALVES
 RUNS = N // SEG
 RUNS_HALF = HALF // SEG
 C_ROW = 4
+SPREAD_STEP = 8
 BIAS_BLOCK = (0, 1)
-K_FIRST = 512
+K_FIRST = 256
+K_ROWS = P - 16
+C_FIRST = 768
 
 
 def tile_attend_questlse_topk_kernel(tc, qT, k_words, k_scales, c_words, c_scales, offs, out):
@@ -40,31 +43,33 @@ def tile_attend_questlse_topk_kernel(tc, qT, k_words, k_scales, c_words, c_scale
         cw_all = sb.tile([P, T], I32, name="cw_all", align_bytes=64)
         ks_all = sb.tile([P, T], U8, name="ks_all", align_bytes=64)
         cs_all = sb.tile([P, T], U8, name="cs_all", align_bytes=64)
-
+        ks_g = sb.tile([P, N], U8, name="ks_g", align_bytes=64)
         cs_g = sb.tile([P, N], U8, name="cs_g", align_bytes=64)
+        ks = sb.tile([P, N], U8, name="ks", align_bytes=64)
         cs = sb.tile([P, N], U8, name="cs", align_bytes=64)
 
-        nc.vector.memset(cs_all[:].bitcast(I32), 0)
-        nc.vector.memset(ks_all[:].bitcast(I32), 0)
-        nc.vector.memset(cs[:].bitcast(I32), 0)
+        def move_rows(queue, plane, first_row, gathered, rows):
+            for r in rows:
+                queue.dma_start(plane[first_row + r:P:32, :].bitcast(I32),
+                                gathered[first_row + SPREAD_STEP * r:P:32, :].bitcast(I32))
+
+        for cleared in (cs_all[:], ks_all[:K_ROWS], ks[:]):
+            nc.vector.memset(cleared.bitcast(I32), 0)
         k_src = k_words[0].rearrange("p t r -> p (t r)").bitcast(I32)
-        nc.sync.dma_start(offsets[:], offs)
-        nc.sync.dma_start(q_raw[:], qT[0].rearrange("(p j) w -> p j w", j=PACK))
-        nc.sync.dma_start(cs_all[C_ROW:P:8, :].bitcast(I32), c_scales[0].bitcast(I32))
         nc.sync.dma_start(kw_all[:, :K_FIRST], k_src[:, :K_FIRST])
-        for r in range(4):
-            nc.sync.dma_start(ks_all[r:P:32, :].bitcast(I32), k_scales[0, r:16:4, :].bitcast(I32))
+        nc.sync.dma_start(offsets[:], offs)
+        nc.sync.dma_start(ks_all[K_ROWS:, :].bitcast(I32), k_scales[0].bitcast(I32))
+        nc.sync.dma_start(q_raw[:], qT[0].rearrange("(p j) w -> p j w", j=PACK))
+        nc.sync.dma_start(cs_all[C_ROW:P:SPREAD_STEP, :].bitcast(I32), c_scales[0].bitcast(I32))
         nc.sync.dma_start(kw_all[:, K_FIRST:], k_src[:, K_FIRST:])
-        nc.sync.dma_start(cw_all[:], c_words[0].rearrange("p t r -> p (t r)").bitcast(I32))
-
-        nc.vector.tensor_copy(cs_g[:], cs_all[:].indirect(offsets[:]))
+        c_src = c_words[0].rearrange("p t r -> p (t r)").bitcast(I32)
+        nc.sync.dma_start(cw_all[:, :C_FIRST], c_src[:, :C_FIRST])
+        nc.vector.tensor_copy(ks_g[:], ks_all[:].indirect(offsets[:]))
         for r in range(4):
-            nc.sync.dma_start(cs[C_ROW + r:P:32, :].bitcast(I32), cs_g[C_ROW + 8 * r:P:32, :].bitcast(I32))
+            nc.sync.dma_start(ks[r:P:32, :].bitcast(I32), ks_g[K_ROWS + r:P:4, :].bitcast(I32))
+        nc.sync.dma_start(cw_all[:, C_FIRST:], c_src[:, C_FIRST:])
 
-        ks = sb.tile([P, N], U8, name="ks", align_bytes=64)
-        nc.vector.tensor_copy(ks[:], ks_all[:].indirect(offsets[:]))
-
-        hi = sb.tile([P, NQ, PACK], BF16, name="hi", align_bytes=64)
+        hi = sb.tile([P, NQ, PACK], BF16, name="hi", tag="hi_then_k", align_bytes=64)
         lo = sb.tile([P, NQ, PACK], BF16, name="lo", align_bytes=64)
         q_read = q_raw[:].rearrange("p j (c i t) -> p t c j i", i=2, t=Q_TILES)
         hi_write = hi[:].rearrange("p (t c i) j -> p t c j i", i=2, t=Q_TILES)
@@ -76,13 +81,17 @@ def tile_attend_questlse_topk_kernel(tc, qT, k_words, k_scales, c_words, c_scale
             nc.scalar.activation(minus_write[:, t], q_read[:, t], ACT.Relu, scale=-1.0)
         nc.scalar.activation(lo[:], minus_lo[:], ACT.Copy, scale=-1.0)
 
-        kw = sb.tile([P, N], U32, name="kw", align_bytes=64)
+        nc.vector.tensor_copy(cs_g[:], cs_all[:].indirect(offsets[:]))
+        nc.vector.tensor_copy(cs[:].bitcast(I32), cs_g[:].bitcast(I32))
+        move_rows(nc.sync, cs, C_ROW, cs_g, range(1, 4))
+
         cw = sb.tile([P, N], U32, name="cw", align_bytes=64)
         hi_s = sb.tile([P, NQ], U8, name="hi_s", align_bytes=64)
         lo_s = sb.tile([P, NQ], U8, name="lo_s", align_bytes=64)
 
         hi_w = sb.tile([P, NQ], U32, name="hi_w", align_bytes=64)
         nc.vector.quantize_mx(out=hi_w[:].bitcast(FP8X4), scales=hi_s[:], in_=hi[:].rearrange("p w j -> p (w j)"))
+        kw = sb.tile([P, N], U32, name="kw", tag="hi_then_k", align_bytes=64)
         for h in range(HALVES):
             nc.vector.tensor_copy(kw[:, h * HALF:(h + 1) * HALF],
                                   kw_all[:].bitcast(U32).indirect(offsets[:, h * HALF // 16:(h + 1) * HALF // 16]))

@@ -28,7 +28,7 @@ SPREAD_STEP = 8
 BIAS_BLOCK = (0, 1)
 K_FIRST = 256
 K_ROWS = P - 16
-C_FIRST = 768
+C_FIRST = 1152
 
 
 def tile_attend_questlse_topk_kernel(tc, qT, k_words, k_scales, c_words, c_scales, offs, out):

@@ -28,7 +28,8 @@ SPREAD_STEP = 8
 BIAS_BLOCK = (0, 1)
 K_FIRST = 256
 K_ROWS = P - 16
-C_FIRST = 1152
+LO_ON_VECTOR = 64
+C_FIRST = 896
 
 
 def tile_attend_questlse_topk_kernel(tc, qT, k_words, k_scales, c_words, c_scales, offs, out):
@@ -39,7 +40,7 @@ def tile_attend_questlse_topk_kernel(tc, qT, k_words, k_scales, c_words, c_scale
 
         offsets = sb.tile([P, N // 16], U16, name="offsets")
         q_raw = sb.tile([P, PACK, NQ], F32, name="q_raw", align_bytes=64)
-        kw_all = sb.tile([P, T], I32, name="kw_all", tag="shared", align_bytes=64)
+        kw_all = sb.tile([P, T], I32, name="kw_all", align_bytes=64)
         cw_all = sb.tile([P, T], I32, name="cw_all", align_bytes=64)
         ks_all = sb.tile([P, T], U8, name="ks_all", align_bytes=64)
         cs_all = sb.tile([P, T], U8, name="cs_all", align_bytes=64)
@@ -73,13 +74,16 @@ def tile_attend_questlse_topk_kernel(tc, qT, k_words, k_scales, c_words, c_scale
         lo = sb.tile([P, NQ, PACK], BF16, name="lo", align_bytes=64)
         q_read = q_raw[:].rearrange("p j (c i t) -> p t c j i", i=2, t=Q_TILES)
         hi_write = hi[:].rearrange("p (t c i) j -> p t c j i", i=2, t=Q_TILES)
+        lo_write = lo[:].rearrange("p (t c i) j -> p t c j i", i=2, t=Q_TILES)
         minus_lo = sb.tile([P, NQ, PACK], BF16, name="minus_lo", align_bytes=64)
         minus_write = minus_lo[:].rearrange("p (t c i) j -> p t c j i", i=2, t=Q_TILES)
+        pairs = LO_ON_VECTOR // 2
         for t in range(Q_TILES):
             nc.scalar.activation(hi_write[:, t], q_read[:, t], ACT.Relu)
-        for t in range(Q_TILES):
-            nc.scalar.activation(minus_write[:, t], q_read[:, t], ACT.Relu, scale=-1.0)
-        nc.scalar.activation(lo[:], minus_lo[:], ACT.Copy, scale=-1.0)
+        nc.vector.tensor_scalar_min(lo_write[:, 0, :pairs], q_read[:, 0, :pairs], 0.0)
+        nc.scalar.activation(minus_write[:, 0, pairs:], q_read[:, 0, pairs:], ACT.Relu, scale=-1.0)
+        nc.scalar.activation(minus_write[:, 1], q_read[:, 1], ACT.Relu, scale=-1.0)
+        nc.scalar.activation(lo[:, LO_ON_VECTOR:], minus_lo[:, LO_ON_VECTOR:], ACT.Copy, scale=-1.0)
 
         nc.vector.tensor_copy(cs_g[:], cs_all[:].indirect(offsets[:]))
         nc.vector.tensor_copy(cs[:].bitcast(I32), cs_g[:].bitcast(I32))
@@ -95,7 +99,7 @@ def tile_attend_questlse_topk_kernel(tc, qT, k_words, k_scales, c_words, c_scale
         for h in range(HALVES):
             nc.vector.tensor_copy(kw[:, h * HALF:(h + 1) * HALF],
                                   kw_all[:].bitcast(U32).indirect(offsets[:, h * HALF // 16:(h + 1) * HALF // 16]))
-        lo_w = sb.tile([P, NQ], U32, name="lo_w", tag="shared", align_bytes=64)
+        lo_w = sb.tile([P, NQ], U32, name="lo_w", align_bytes=64)
         nc.vector.quantize_mx(out=lo_w[:].bitcast(FP8X4), scales=lo_s[:], in_=lo[:].rearrange("p w j -> p (w j)"))
 
         blocks = [(h, t) for h in range(HALVES) for t in range(Q_TILES)]

@@ -102,41 +102,59 @@ def tile_attend_questlse_topk_kernel(tc, qT, k_words, k_scales, c_words, c_scale
         lo_w = sb.tile([P, NQ], U32, name="lo_w", align_bytes=64)
         nc.vector.quantize_mx(out=lo_w[:].bitcast(FP8X4), scales=lo_s[:], in_=lo[:].rearrange("p w j -> p (w j)"))
 
-        blocks = [(h, t) for h in range(HALVES) for t in range(Q_TILES)]
-        acc = {b: ps.tile([P, HALF], F32, name="acc%d%d" % b) for b in blocks}
-        for h, t in blocks:
-            qs = slice(t * P, (t + 1) * P)
-            ns = slice(h * HALF, (h + 1) * HALF)
-            nc.tensor.matmul_mx(out=acc[h, t][:], lhsT=hi_w[:, qs].bitcast(FP8X4), lhsT_scale=hi_s[:, qs],
-                                rhs=kw[:, ns].bitcast(FP8X4), rhs_scale=ks[:, ns], start=True, stop=False)
+        banks = [(0, 0, 128), (0, 128, 128), (1, 0, 128), (1, 128, 128), (0, 256, 256), (1, 256, 128), (1, 384, 128)]
+        by_bias = (0, 1, 2)
+        acc = [ps.tile([P, width], F32, name="acc%d" % b) for b, (t, first, width) in enumerate(banks)]
+
+        def multiply(b, codes, scales, words, plane, opens):
+            t, first, width = banks[b]
+            qs, ns = slice(t * P, (t + 1) * P), slice(first, first + width)
+            nc.tensor.matmul_mx(out=acc[b][:], lhsT=codes[:, qs].bitcast(FP8X4), lhsT_scale=scales[:, qs],
+                                rhs=words[:, ns].bitcast(FP8X4), rhs_scale=plane[:, ns], start=opens, stop=not opens)
+
+        for b in range(len(banks)):
+            multiply(b, hi_w, hi_s, kw, ks, True)
         for h in range(HALVES):
             ns = slice(h * HALF, (h + 1) * HALF)
             nc.vector.tensor_copy(cw[:, ns], cw_all[:].bitcast(U32).indirect(offsets[:, h * HALF // 16:(h + 1) * HALF // 16]))
-            for t in range(Q_TILES):
-                qs = slice(t * P, (t + 1) * P)
-                nc.tensor.matmul_mx(out=acc[h, t][:], lhsT=lo_w[:, qs].bitcast(FP8X4), lhsT_scale=lo_s[:, qs],
-                                    rhs=cw[:, ns].bitcast(FP8X4), rhs_scale=cs[C_ROW:, ns], start=False, stop=True)
+            for b, (t, first, width) in enumerate(banks):
+                if first // HALF == h:
+                    multiply(b, lo_w, lo_s, cw, cs[C_ROW:], False)
 
         top = sb.tile([P, Q_TILES, RUNS], F32, name="top")
         total = sb.tile([P, Q_TILES, RUNS], F32, name="total")
-        shifted = {b: sb.tile([P, RUNS_HALF, SEG], F32, name="shifted%d%d" % b) for b in blocks if b != BIAS_BLOCK}
-        weight = {b: sb.tile([P, RUNS_HALF, SEG], F32, name="weight%d%d" % b) for b in blocks}
-        runs = {b: acc[b][:].rearrange("p (j s) -> p j s", s=SEG) for b in blocks}
-        for h in range(HALVES):
-            js = slice(h * RUNS_HALF, (h + 1) * RUNS_HALF)
-            for t in range(Q_TILES):
-                nc.vector.tensor_reduce(top[:, t, js], runs[h, t], AX.X, ALU.max, negate=True)
-                if (h, t) == BIAS_BLOCK:
-                    for j in range(RUNS_HALF):
-                        nc.scalar.activation(weight[h, t][:, j, :], runs[h, t][:, j, :], ACT.Exp, bias=top[:, t, j:j + 1])
-            for t in range(Q_TILES):
-                if (h, t) != BIAS_BLOCK:
-                    nc.vector.tensor_tensor(shifted[h, t][:], runs[h, t],
-                                            top[:, t, js].unsqueeze(2).to_broadcast([P, RUNS_HALF, SEG]), ALU.add)
-                    nc.scalar.activation(weight[h, t][:], shifted[h, t][:], ACT.Exp)
-        for h, t in blocks:
-            js = slice(h * RUNS_HALF, (h + 1) * RUNS_HALF)
-            nc.vector.tensor_reduce(total[:, t, js], weight[h, t][:], AX.X, ALU.add)
+        weight = [sb.tile([P, width // SEG, SEG], F32, name="weight%d" % b) for b, (t, first, width) in enumerate(banks)]
+        runs = [acc[b][:].rearrange("p (j s) -> p j s", s=SEG) for b in range(len(banks))]
+
+        def of_bank(tile, b):
+            t, first, width = banks[b]
+            return tile[:, t, first // SEG:(first + width) // SEG]
+
+        def maximum(b):
+            nc.vector.tensor_reduce(of_bank(top, b), runs[b], AX.X, ALU.max, negate=True)
+            if b in by_bias:
+                for j in range(banks[b][2] // SEG):
+                    nc.scalar.activation(weight[b][:, j, :], runs[b][:, j, :], ACT.Exp, bias=of_bank(top, b)[:, j:j + 1])
+
+        def shift(b):
+            shape = [P, banks[b][2] // SEG, SEG]
+            shifted = sb.tile(shape, F32, name="shifted%d" % b)
+            nc.vector.tensor_tensor(shifted[:], runs[b], of_bank(top, b).unsqueeze(2).to_broadcast(shape), ALU.add)
+            nc.scalar.activation(weight[b][:], shifted[:], ACT.Exp)
+
+        maximum(0)
+        maximum(1)
+        maximum(2)
+        maximum(3)
+        shift(3)
+        maximum(4)
+        maximum(5)
+        shift(4)
+        maximum(6)
+        shift(5)
+        shift(6)
+        for b in range(len(banks)):
+            nc.vector.tensor_reduce(of_bank(total, b), weight[b][:], AX.X, ALU.add)
         logs = sb.tile([P, Q_TILES, RUNS], F32, name="logs")
         result = sb.tile([P, Q_TILES, RUNS], F32, name="result")
         nc.scalar.activation(logs[:], total[:], ACT.Ln)

@@ -72,18 +72,19 @@ def tile_attend_questlse_topk_kernel(tc, qT, k_words, k_scales, c_words, c_scale
 
         hi = sb.tile([P, NQ, PACK], BF16, name="hi", tag="hi_then_k", align_bytes=64)
         lo = sb.tile([P, NQ, PACK], BF16, name="lo", align_bytes=64)
-        q_read = q_raw[:].rearrange("p j (c i t) -> p t c j i", i=2, t=Q_TILES)
-        hi_write = hi[:].rearrange("p (t c i) j -> p t c j i", i=2, t=Q_TILES)
-        lo_write = lo[:].rearrange("p (t c i) j -> p t c j i", i=2, t=Q_TILES)
         minus_lo = sb.tile([P, NQ, PACK], BF16, name="minus_lo", align_bytes=64)
-        minus_write = minus_lo[:].rearrange("p (t c i) j -> p t c j i", i=2, t=Q_TILES)
-        pairs = LO_ON_VECTOR // 2
-        for t in range(Q_TILES):
-            nc.scalar.activation(hi_write[:, t], q_read[:, t], ACT.Relu)
-        nc.vector.tensor_scalar_min(lo_write[:, 0, :pairs], q_read[:, 0, :pairs], 0.0)
-        nc.scalar.activation(minus_write[:, 0, pairs:], q_read[:, 0, pairs:], ACT.Relu, scale=-1.0)
-        nc.scalar.activation(minus_write[:, 1], q_read[:, 1], ACT.Relu, scale=-1.0)
-        nc.scalar.activation(lo[:, LO_ON_VECTOR:], minus_lo[:, LO_ON_VECTOR:], ACT.Copy, scale=-1.0)
+
+        def rows_of(queries):
+            return q_raw[:, :, queries].rearrange("p j (c i) -> p c j i", i=4)
+
+        def woven(tile, queries):
+            return tile[:, queries].rearrange("p (c i) j -> p c j i", i=4)
+
+        every, first, rest = slice(0, NQ), slice(0, LO_ON_VECTOR), slice(LO_ON_VECTOR, NQ)
+        nc.scalar.activation(woven(hi, every), rows_of(every), ACT.Relu)
+        nc.vector.tensor_scalar_min(woven(lo, first), rows_of(first), 0.0)
+        nc.scalar.activation(woven(minus_lo, rest), rows_of(rest), ACT.Relu, scale=-1.0)
+        nc.scalar.activation(lo[:, rest], minus_lo[:, rest], ACT.Copy, scale=-1.0)
 
         nc.vector.tensor_copy(cs_g[:], cs_all[:].indirect(offsets[:]))
         nc.vector.tensor_copy(cs[:].bitcast(I32), cs_g[:].bitcast(I32))
@@ -102,7 +103,7 @@ def tile_attend_questlse_topk_kernel(tc, qT, k_words, k_scales, c_words, c_scale
         lo_w = sb.tile([P, NQ], U32, name="lo_w", align_bytes=64)
         nc.vector.quantize_mx(out=lo_w[:].bitcast(FP8X4), scales=lo_s[:], in_=lo[:].rearrange("p w j -> p (w j)"))
 
-        banks = [(0, 0, 128), (0, 128, 128), (1, 0, 128), (1, 128, 128), (0, 256, 256), (1, 256, 128), (1, 384, 128)]
+        banks = [(0, 0, 128), (0, 128, 128), (1, 0, 256), (0, 256, 256), (1, 256, 128), (1, 384, 128)]
         by_bias = (0, 1, 2)
         acc = [ps.tile([P, width], F32, name="acc%d" % b) for b, (t, first, width) in enumerate(banks)]
 
@@ -146,17 +147,15 @@ def tile_attend_questlse_topk_kernel(tc, qT, k_words, k_scales, c_words, c_scale
         maximum(1)
         maximum(2)
         maximum(3)
-        shift(3)
         maximum(4)
+        shift(3)
         maximum(5)
         shift(4)
-        maximum(6)
         shift(5)
-        shift(6)
         for b in range(len(banks)):
             nc.vector.tensor_reduce(of_bank(total, b), weight[b][:], AX.X, ALU.add)
         logs = sb.tile([P, Q_TILES, RUNS], F32, name="logs")
         result = sb.tile([P, Q_TILES, RUNS], F32, name="result")
         nc.scalar.activation(logs[:], total[:], ACT.Ln)
         nc.vector.tensor_tensor(result[:], logs[:], top[:], ALU.subtract)
-        nc.sync.dma_start(out[0].rearrange("(p t) j -> p t j", t=Q_TILES), result[:])
+        nc.sync.dma_start(out[0].rearrange("(t p) j -> p t j", t=Q_TILES), result[:])

@@ -113,6 +113,9 @@ def tile_attend_questlse_topk_kernel(tc, qT, k_words, k_scales, c_words, c_scale
             nc.tensor.matmul_mx(out=acc[b][:], lhsT=codes[:, qs].bitcast(FP8X4), lhsT_scale=scales[:, qs],
                                 rhs=words[:, ns].bitcast(FP8X4), rhs_scale=plane[:, ns], start=opens, stop=not opens)
 
+        warm = ps.tile([P, NQ], F32, name="warm")
+        nc.tensor.matmul_mx(out=warm[:], lhsT=hi_w[:, :P].bitcast(FP8X4), lhsT_scale=hi_s[:, :P],
+                            rhs=hi_w[:].bitcast(FP8X4), rhs_scale=hi_s[:], start=True, stop=True)
         for b in range(len(banks)):
             multiply(b, hi_w, hi_s, kw, ks, True)
         for h in range(HALVES):

from contextlib import ExitStack

import concourse.mybir as mybir

D, T, N, NQ, SEG = 512, 2048, 512, 256, 16
FLOPS = 2 * 2 * NQ * D * N

F32 = mybir.dt.float32
BF16 = mybir.dt.bfloat16
I32 = mybir.dt.int32
U32 = mybir.dt.uint32
U16 = mybir.dt.uint16
U8 = mybir.dt.uint8
FP8X4 = mybir.dt.float8_e4m3fn_x4
ALU = mybir.AluOpType
ACT = mybir.ActivationFunctionType
AX = mybir.AxisListType

P = 128
PACK = 4
Q_TILES = NQ // P
HALVES = 2
HALF = N // HALVES
RUNS = N // SEG
RUNS_HALF = HALF // SEG
C_ROW = 4
SPREAD_STEP = 8
BIAS_BLOCK = (0, 1)
K_FIRST = 256
K_ROWS = P - 16
LO_ON_VECTOR = 64
C_FIRST = 896


def tile_attend_questlse_topk_kernel(tc, qT, k_words, k_scales, c_words, c_scales, offs, out):
    nc = tc.nc
    with ExitStack() as ctx:
        sb = ctx.enter_context(tc.tile_pool(name="sb", bufs=1))
        ps = ctx.enter_context(tc.psum_pool(name="ps", bufs=1))

        offsets = sb.tile([P, N // 16], U16, name="offsets")
        q_raw = sb.tile([P, PACK, NQ], F32, name="q_raw", align_bytes=64)
        kw_all = sb.tile([P, T], I32, name="kw_all", align_bytes=64)
        cw_all = sb.tile([P, T], I32, name="cw_all", align_bytes=64)
        ks_all = sb.tile([P, T], U8, name="ks_all", align_bytes=64)
        cs_all = sb.tile([P, T], U8, name="cs_all", align_bytes=64)
        ks_g = sb.tile([P, N], U8, name="ks_g", align_bytes=64)
        cs_g = sb.tile([P, N], U8, name="cs_g", align_bytes=64)
        ks = sb.tile([P, N], U8, name="ks", align_bytes=64)
        cs = sb.tile([P, N], U8, name="cs", align_bytes=64)

        def move_rows(queue, plane, first_row, gathered, rows):
            for r in rows:
                queue.dma_start(plane[first_row + r:P:32, :].bitcast(I32),
                                gathered[first_row + SPREAD_STEP * r:P:32, :].bitcast(I32))

        for cleared in (cs_all[:], ks_all[:K_ROWS], ks[:]):
            nc.vector.memset(cleared.bitcast(I32), 0)
        k_src = k_words[0].rearrange("p t r -> p (t r)").bitcast(I32)
        nc.sync.dma_start(kw_all[:, :K_FIRST], k_src[:, :K_FIRST])
        nc.sync.dma_start(offsets[:], offs)
        nc.sync.dma_start(ks_all[K_ROWS:, :].bitcast(I32), k_scales[0].bitcast(I32))
        nc.sync.dma_start(q_raw[:], qT[0].rearrange("(p j) w -> p j w", j=PACK))
        nc.sync.dma_start(cs_all[C_ROW:P:SPREAD_STEP, :].bitcast(I32), c_scales[0].bitcast(I32))
        nc.sync.dma_start(kw_all[:, K_FIRST:], k_src[:, K_FIRST:])
        c_src = c_words[0].rearrange("p t r -> p (t r)").bitcast(I32)
        nc.sync.dma_start(cw_all[:, :C_FIRST], c_src[:, :C_FIRST])
        nc.vector.tensor_copy(ks_g[:], ks_all[:].indirect(offsets[:]))
        for r in range(4):
            nc.sync.dma_start(ks[r:P:32, :].bitcast(I32), ks_g[K_ROWS + r:P:4, :].bitcast(I32))
        nc.sync.dma_start(cw_all[:, C_FIRST:], c_src[:, C_FIRST:])

        hi = sb.tile([P, NQ, PACK], BF16, name="hi", tag="hi_then_k", align_bytes=64)
        lo = sb.tile([P, NQ, PACK], BF16, name="lo", align_bytes=64)
        minus_lo = sb.tile([P, NQ, PACK], BF16, name="minus_lo", align_bytes=64)

        def rows_of(queries):
            return q_raw[:, :, queries].rearrange("p j (c i) -> p c j i", i=4)

        def woven(tile, queries):
            return tile[:, queries].rearrange("p (c i) j -> p c j i", i=4)

        every, first, rest = slice(0, NQ), slice(0, LO_ON_VECTOR), slice(LO_ON_VECTOR, NQ)
        nc.scalar.activation(woven(hi, every), rows_of(every), ACT.Relu)
        nc.vector.tensor_scalar_min(woven(lo, first), rows_of(first), 0.0)
        nc.scalar.activation(woven(minus_lo, rest), rows_of(rest), ACT.Relu, scale=-1.0)
        nc.scalar.activation(lo[:, rest], minus_lo[:, rest], ACT.Copy, scale=-1.0)

        nc.vector.tensor_copy(cs_g[:], cs_all[:].indirect(offsets[:]))
        nc.vector.tensor_copy(cs[:].bitcast(I32), cs_g[:].bitcast(I32))
        move_rows(nc.sync, cs, C_ROW, cs_g, range(1, 4))

        cw = sb.tile([P, N], U32, name="cw", align_bytes=64)
        hi_s = sb.tile([P, NQ], U8, name="hi_s", align_bytes=64)
        lo_s = sb.tile([P, NQ], U8, name="lo_s", align_bytes=64)

        hi_w = sb.tile([P, NQ], U32, name="hi_w", align_bytes=64)
        nc.vector.quantize_mx(out=hi_w[:].bitcast(FP8X4), scales=hi_s[:], in_=hi[:].rearrange("p w j -> p (w j)"))
        kw = sb.tile([P, N], U32, name="kw", tag="hi_then_k", align_bytes=64)
        for h in range(HALVES):
            nc.vector.tensor_copy(kw[:, h * HALF:(h + 1) * HALF],
                                  kw_all[:].bitcast(U32).indirect(offsets[:, h * HALF // 16:(h + 1) * HALF // 16]))
        lo_w = sb.tile([P, NQ], U32, name="lo_w", align_bytes=64)
        nc.vector.quantize_mx(out=lo_w[:].bitcast(FP8X4), scales=lo_s[:], in_=lo[:].rearrange("p w j -> p (w j)"))

        banks = [(0, 0, 128), (0, 128, 128), (1, 0, 256), (0, 256, 256), (1, 256, 128), (1, 384, 128)]
        by_bias = (0, 1, 2)
        acc = [ps.tile([P, width], F32, name="acc%d" % b) for b, (t, first, width) in enumerate(banks)]

        def multiply(b, codes, scales, words, plane, opens):
            t, first, width = banks[b]
            qs, ns = slice(t * P, (t + 1) * P), slice(first, first + width)
            nc.tensor.matmul_mx(out=acc[b][:], lhsT=codes[:, qs].bitcast(FP8X4), lhsT_scale=scales[:, qs],
                                rhs=words[:, ns].bitcast(FP8X4), rhs_scale=plane[:, ns], start=opens, stop=not opens)

        warm = ps.tile([P, NQ], F32, name="warm")
        nc.tensor.matmul_mx(out=warm[:], lhsT=hi_w[:, :P].bitcast(FP8X4), lhsT_scale=hi_s[:, :P],
                            rhs=hi_w[:].bitcast(FP8X4), rhs_scale=hi_s[:], start=True, stop=True)
        for b in range(len(banks)):
            multiply(b, hi_w, hi_s, kw, ks, True)
        for h in range(HALVES):
            ns = slice(h * HALF, (h + 1) * HALF)
            nc.vector.tensor_copy(cw[:, ns], cw_all[:].bitcast(U32).indirect(offsets[:, h * HALF // 16:(h + 1) * HALF // 16]))
            for b, (t, first, width) in enumerate(banks):
                if first // HALF == h:
                    multiply(b, lo_w, lo_s, cw, cs[C_ROW:], False)

        top = sb.tile([P, Q_TILES, RUNS], F32, name="top")
        total = sb.tile([P, Q_TILES, RUNS], F32, name="total")
        weight = [sb.tile([P, width // SEG, SEG], F32, name="weight%d" % b) for b, (t, first, width) in enumerate(banks)]
        runs = [acc[b][:].rearrange("p (j s) -> p j s", s=SEG) for b in range(len(banks))]

        def of_bank(tile, b):
            t, first, width = banks[b]
            return tile[:, t, first // SEG:(first + width) // SEG]

        def maximum(b):
            nc.vector.tensor_reduce(of_bank(top, b), runs[b], AX.X, ALU.max, negate=True)
            if b in by_bias:
                for j in range(banks[b][2] // SEG):
                    nc.scalar.activation(weight[b][:, j, :], runs[b][:, j, :], ACT.Exp, bias=of_bank(top, b)[:, j:j + 1])

        def shift(b):
            shape = [P, banks[b][2] // SEG, SEG]
            shifted = sb.tile(shape, F32, name="shifted%d" % b)
            nc.vector.tensor_tensor(shifted[:], runs[b], of_bank(top, b).unsqueeze(2).to_broadcast(shape), ALU.add)
            nc.scalar.activation(weight[b][:], shifted[:], ACT.Exp)

        maximum(0)
        maximum(1)
        maximum(2)
        maximum(3)
        maximum(4)
        shift(3)
        maximum(5)
        shift(4)
        shift(5)
        for b in range(len(banks)):
            nc.vector.tensor_reduce(of_bank(total, b), weight[b][:], AX.X, ALU.add)
        logs = sb.tile([P, Q_TILES, RUNS], F32, name="logs")
        result = sb.tile([P, Q_TILES, RUNS], F32, name="result")
        nc.scalar.activation(logs[:], total[:], ACT.Ln)
        nc.vector.tensor_tensor(result[:], logs[:], top[:], ALU.subtract)
        nc.sync.dma_start(out[0].rearrange("(t p) j -> p t j", t=Q_TILES), result[:])
